import numpy as np, ml_dtypes
CORES = [26,28,98,100,106,108,122,124]
N = 8
TK = 512
COEF = [[3,1,1,1,1,1,1,1],[1,3,1,1,1,1,1,1],[1,1,3,1,1,1,1,1],[1,1,1,3,1,1,1,1],[1,1,1,1,3,1,1,1],[1,1,1,1,1,3,1,1],[1,1,1,1,1,1,3,1],[1,1,1,1,1,1,1,3]]
def setup_inputs(rng):
    return {"x": rng.standard_normal((N, 128, TK), dtype=np.float32).astype(ml_dtypes.bfloat16), "a": (rng.standard_normal((N, 128, 128), dtype=np.float32) / 11).astype(ml_dtypes.bfloat16)}
def setup_inputs_big(rng):
    d = setup_inputs(rng)
    for k in ("x", "a"): d[k] = (d[k].astype(np.float32) * 1024.0).astype(d[k].dtype)
    return d
def setup_inputs_small(rng):
    d = setup_inputs(rng)
    for k in ("x", "a"): d[k] = (d[k].astype(np.float32) * (1 / 1024.0)).astype(d[k].dtype)
    return d
def setup_inputs_apart(rng):
    d = setup_inputs(rng)
    f = (10.0 ** rng.permutation(np.linspace(-1.5, 1.5, N))).astype(np.float32).reshape(N, 1, 1)
    for k in ("x", "a"): d[k] = (d[k].astype(np.float32) * f).astype(d[k].dtype)
    return d
def reference(x, a):
    X, A = x.astype(np.float64), a.astype(np.float64)
    y = np.stack([A[r].T @ sum(COEF[r][j] * X[j] for j in range(N)) for r in range(N)])
    return {"y": y.astype(ml_dtypes.bfloat16)}

@@ -1,0 +1,177 @@
+from concourse.bass import DstId, RemoteDMATransfer
+
+WID = 512
+HALF = 256
+NSLOT = 40
+TWOHOP_DIRECT = False
+HELP = False
+NE = 8
+NE_LONE = 16
+
+SCRATCH = {
+    "xs": ("sbuf", [128, WID], "bfloat16"),
+    "aw": ("sbuf", [128, 128], "bfloat16"),
+    "land": ("sbuf", [128, NSLOT * WID], "bfloat16"),
+    "yb": ("sbuf", [128, WID], "bfloat16"),
+    "ps0": ("psum", [128, 512], "float32"),
+    "ps1": ("psum", [128, 512], "float32"),
+}
+SEMAPHORES = ["ldx", "lda", "sent", "mm0", "mm1", "cp0", "cp1", "st0", "st1"] + ["m%d" % i for i in range(NSLOT)]
+
+
+def make_plan(cores, topo):
+    chips = sorted({topo.chip(c) for c in cores})
+    on = {X: sorted(c for c in cores if topo.chip(c) == X) for X in chips}
+    msgs = []
+
+    def add(src, parts, c0, c1, dsts, stage, ne):
+        msgs.append(dict(id=len(msgs), src=src, parts=list(parts), c0=c0, c1=c1, dsts=list(dsts), stage=stage, ne=ne))
+        return len(msgs) - 1
+
+    def is_open(X, Y):
+        return all(topo.may_write(s, d) for s in on[X] for d in on[Y])
+
+    def peers(c):
+        return [p for p in on[topo.chip(c)] if p != c]
+
+    gated = {X: [Y for Y in chips if Y != X and not is_open(X, Y)] for X in chips}
+    free = {X: [Y for Y in chips if Y != X and is_open(X, Y)] for X in chips}
+    exps, helpers = {}, {}
+    for X in chips:
+        far = [d for Y in gated[X] for d in on[Y]]
+        exps[X] = [s for s in on[X] if all(topo.may_write(s, d) for d in far)]
+        helpers[X] = []
+        if HELP and far and not free[X]:
+            dies = {topo.die(s) for s in exps[X]}
+            for h in range(topo.CHIPS * topo.CORES_PER_CHIP):
+                if topo.chip(h) == X and h not in cores and topo.die(h) not in dies \
+                        and all(topo.may_write(h, d) for d in far):
+                    helpers[X].append(h)
+                    dies.add(topo.die(h))
+    loc, rawin, halfin = {}, {c: [] for c in cores}, {c: [] for c in cores}
+    for s in cores:
+        X = topo.chip(s)
+        loc[s] = add(s, ["x"], 0, WID, peers(s) + helpers[X], 1.0, NE if free[X] else NE_LONE)
+    for s in cores:
+        dsts = [d for Y in free[topo.chip(s)] for d in on[Y] if topo.die(d) == topo.die(s)]
+        if dsts:
+            m = add(s, ["x"], 0, WID, dsts, 1.5, NE)
+            for d in dsts:
+                rawin[d].append(m)
+    for X in chips:
+        ex = exps[X] + helpers[X]
+        if not gated[X]:
+            continue
+
+        def parts(e):
+            return (["x"] if e in cores else []) + [loc[s] for s in on[X] if s != e]
+        halves = [Y for Y in gated[X] if not (TWOHOP_DIRECT or topo.mates(X, Y))]
+        direct = [d for Y in gated[X] if Y not in halves for d in on[Y]]
+        if halves:
+            for k in range(2):
+                dsts = [on[Y][k] for Y in halves]
+                e = ex[k % len(ex)]
+                m = add(e, parts(e), k * HALF, (k + 1) * HALF, dsts, 2.0, NE // 2 if len(ex) == 1 else NE)
+                for d in dsts:
+                    halfin[d].append(m)
+        for i, e in enumerate(ex):
+            dsts = direct[i::len(ex)]
+            if dsts:
+                add(e, parts(e), 0, WID, dsts, 2.7 if halves else 2.5, NE)
+    for d in cores:
+        if rawin[d]:
+            add(d, rawin[d], 0, WID, peers(d), 2.6, NE)
+    for d in cores:
+        if halfin[d]:
+            h = msgs[halfin[d][0]]
+            add(d, halfin[d], h["c0"], h["c1"], peers(d), 3.0, NE)
+    assert len(msgs) <= NSLOT
+    return msgs
+
+
+def rank_program(g, core, T, topo):
+    cores = list(T.cores)
+    msgs = make_plan(cores, topo)
+    mine = [m for m in msgs if m["src"] == core]
+    rank = T.rank_of(core)
+    if rank is None and not mine:
+        return
+    sem = T.sem
+
+    def msem(i):
+        return sem["m%d" % i]
+
+    def piece(p, c0, c1):
+        return T.xs[:, c0:c1] if p == "x" else T.land[:, p * WID + c0:p * WID + c1]
+
+    if rank is not None:
+        g.sync.dma_start(T.xs[:], T.x[:]).then_inc(sem.ldx, 16)
+        g.scalar.dma_start(T.aw[:], T.a[:]).then_inc(sem.lda, 16)
+
+    def key(m):
+        return 1.0 if m["stage"] < 2 else m["stage"]
+    seen, total = set(), 0
+    for k in sorted({key(m) for m in mine}):
+        grp = [m for m in mine if key(m) == k]
+        for m in grp:
+            for p in m["parts"]:
+                if p not in seen:
+                    seen.add(p)
+                    if p == "x":
+                        g.wait_ge(sem.ldx, 16)
+                    else:
+                        g.wait_ge(msem(p), msgs[p]["ne"])
+        used, trs = set(), []
+        for m in sorted(grp, key=lambda m: all(topo.chip(d) == topo.chip(core) for d in m["dsts"])):
+            allowed = None
+            for d in m["dsts"]:
+                assert topo.may_write(core, d)
+                allowed = topo.mask(core, d) if allowed is None else allowed & topo.mask(core, d)
+            idle = [b for b in range(allowed.bit_length()) if (allowed >> b) & 1 and b not in used]
+            local = all(topo.chip(d) == topo.chip(core) for d in m["dsts"])
+            sel = idle[-m["ne"]:] if local else idle[:m["ne"]]
+            assert len(sel) == m["ne"]
+            used.update(sel)
+            srcs = [piece(p, m["c0"], m["c1"]) for p in m["parts"]]
+            trs.append(RemoteDMATransfer(
+                dst_ids=[DstId(rid=topo.addr(d)[0], pnc=topo.addr(d)[1]) for d in m["dsts"]],
+                dma_engine_mask=sum(1 << b for b in sel), remote_sem=msem(m["id"]), srcs=srcs,
+                dsts=[piece(m["id"], m["c0"], m["c1"]) for d in m["dsts"]], alu_op=1 if len(srcs) > 1 else 0))
+            total += m["ne"]
+        g.remote_dma_fused(trs, local_sem=sem.sent)
+
+    if rank is not None:
+        coef = T.tables["COEF"][rank]
+        assert all(coef[j] == 1 for j in range(len(cores)) if j != rank) and coef[rank] >= 1
+        jobs = [(None, "x", b) for _ in range(coef[rank]) for b in range(2)]
+        for m in sorted((m for m in msgs if core in m["dsts"]), key=lambda m: (m["stage"], m["id"])):
+            for b in range(2):
+                if m["c0"] <= b * HALF and (b + 1) * HALF <= m["c1"]:
+                    jobs.append((m, m["id"], b))
+        ps = [T.ps0, T.ps1]
+        count = [sum(1 for j in jobs if j[2] == b) for b in range(2)]
+        done, waited, order = [0, 0], set(), []
+        t = g.tensor
+        t.wait_ge(sem.lda, 16)
+        t.wait_ge(sem.ldx, 16)
+        for m, p, b in jobs:
+            if m is not None and p not in waited:
+                waited.add(p)
+                t.wait_ge(msem(p), m["ne"])
+            ins = t.matmul(ps[b][:, 0:HALF], T.aw[:], piece(p, b * HALF, (b + 1) * HALF),
+                           done[b] == 0, done[b] == count[b] - 1)
+            done[b] += 1
+            if done[b] == count[b]:
+                ins.then_inc(sem["mm%d" % b], 1)
+                order.append(b)
+        for q, b in zip((g.sync, g.scalar), order):
+            cols = slice(b * HALF, (b + 1) * HALF)
+            g.vector.wait_ge(sem["mm%d" % b], 1)
+            g.vector.tensor_copy(T.yb[:, cols], ps[b][:, 0:HALF]).then_inc(sem["cp%d" % b], 1)
+            q.wait_ge(sem["cp%d" % b], 1)
+            q.dma_start(T.y[:, cols], T.yb[:, cols]).then_inc(sem["st%d" % b], 16)
+    if total:
+        g.wait_ge(sem.sent, total)
+    if rank is not None:
+        g.wait_ge(sem.st0, 16)
+        g.wait_ge(sem.st1, 16)

@@ -2,16 +2,12 @@ from concourse.bass import DstId, RemoteDMATransfer
 
 WID = 512
 HALF = 256
-NSLOT = 40
-TWOHOP_DIRECT = False
-HELP = False
-NE = 8
-NE_LONE = 16
+NSLOT = 32
 
 SCRATCH = {
     "xs": ("sbuf", [128, WID], "bfloat16"),
     "aw": ("sbuf", [128, 128], "bfloat16"),
-    "land": ("sbuf", [128, NSLOT * WID], "bfloat16"),
+    "land": ("sbuf", [128, NSLOT * HALF], "bfloat16"),
     "yb": ("sbuf", [128, WID], "bfloat16"),
     "ps0": ("psum", [128, 512], "float32"),
     "ps1": ("psum", [128, 512], "float32"),
@@ -21,70 +17,56 @@ SEMAPHORES = ["ldx", "lda", "sent", "mm0", "mm1", "cp0", "cp1", "st0", "st1"] + 
 
 def make_plan(cores, topo):
     chips = sorted({topo.chip(c) for c in cores})
-    on = {X: sorted(c for c in cores if topo.chip(c) == X) for X in chips}
+    own = {X: sorted((c for c in cores if topo.chip(c) == X), key=topo.die) for X in chips}
+    assert all(len(own[X]) == 2 and [topo.die(c) for c in own[X]] == [topo.die(c) for c in own[chips[0]]]
+               for X in chips)
     msgs = []
 
-    def add(src, parts, c0, c1, dsts, stage, ne):
-        msgs.append(dict(id=len(msgs), src=src, parts=list(parts), c0=c0, c1=c1, dsts=list(dsts), stage=stage, ne=ne))
+    def engines(src, dsts):
+        m = None
+        for d in dsts:
+            m = topo.mask(src, d) if m is None else m & topo.mask(src, d)
+        return bin(m).count("1")
+
+    def add(src, parts, k, dsts, stage, share=1):
+        msgs.append(dict(id=len(msgs), src=src, parts=list(parts), k=k, dsts=list(dsts), stage=stage,
+                         ne=engines(src, dsts) // share))
         return len(msgs) - 1
 
-    def is_open(X, Y):
-        return all(topo.may_write(s, d) for s in on[X] for d in on[Y])
-
-    def peers(c):
-        return [p for p in on[topo.chip(c)] if p != c]
-
-    gated = {X: [Y for Y in chips if Y != X and not is_open(X, Y)] for X in chips}
-    free = {X: [Y for Y in chips if Y != X and is_open(X, Y)] for X in chips}
-    exps, helpers = {}, {}
+    shut, helper = {}, {}
     for X in chips:
-        far = [d for Y in gated[X] for d in on[Y]]
-        exps[X] = [s for s in on[X] if all(topo.may_write(s, d) for d in far)]
-        helpers[X] = []
-        if HELP and far and not free[X]:
-            dies = {topo.die(s) for s in exps[X]}
-            for h in range(topo.CHIPS * topo.CORES_PER_CHIP):
-                if topo.chip(h) == X and h not in cores and topo.die(h) not in dies \
-                        and all(topo.may_write(h, d) for d in far):
-                    helpers[X].append(h)
-                    dies.add(topo.die(h))
-    loc, rawin, halfin = {}, {c: [] for c in cores}, {c: [] for c in cores}
-    for s in cores:
-        X = topo.chip(s)
-        loc[s] = add(s, ["x"], 0, WID, peers(s) + helpers[X], 1.0, NE if free[X] else NE_LONE)
-    for s in cores:
-        dsts = [d for Y in free[topo.chip(s)] for d in on[Y] if topo.die(d) == topo.die(s)]
-        if dsts:
-            m = add(s, ["x"], 0, WID, dsts, 1.5, NE)
-            for d in dsts:
-                rawin[d].append(m)
+        for k in range(2):
+            o = own[X][k]
+            shut[X, k] = [own[Y][k] for Y in chips if Y != X and not topo.may_write(o, own[Y][k])]
+            if shut[X, k]:
+                helper[X, k] = next(h for h in range(topo.CHIPS * topo.CORES_PER_CHIP)
+                                    if topo.chip(h) == X and h not in cores and topo.die(h) == topo.die(o)
+                                    and all(topo.may_write(h, d) for d in shut[X, k]))
+    at = {}
     for X in chips:
-        ex = exps[X] + helpers[X]
-        if not gated[X]:
-            continue
-
-        def parts(e):
-            return (["x"] if e in cores else []) + [loc[s] for s in on[X] if s != e]
-        halves = [Y for Y in gated[X] if not (TWOHOP_DIRECT or topo.mates(X, Y))]
-        direct = [d for Y in gated[X] if Y not in halves for d in on[Y]]
-        if halves:
-            for k in range(2):
-                dsts = [on[Y][k] for Y in halves]
-                e = ex[k % len(ex)]
-                m = add(e, parts(e), k * HALF, (k + 1) * HALF, dsts, 2.0, NE // 2 if len(ex) == 1 else NE)
+        for k in range(2):
+            s = own[X][k]
+            outs = [(1 - k, [own[X][1 - k]] + ([helper[X, 1 - k]] if (X, 1 - k) in helper else []))]
+            if (X, k) in helper:
+                outs.append((k, [helper[X, k]]))
+            for kk, dsts in outs:
+                m = add(s, ["x"], kk, dsts, 1.0, len(outs))
                 for d in dsts:
-                    halfin[d].append(m)
-        for i, e in enumerate(ex):
-            dsts = direct[i::len(ex)]
-            if dsts:
-                add(e, parts(e), 0, WID, dsts, 2.7 if halves else 2.5, NE)
-    for d in cores:
-        if rawin[d]:
-            add(d, rawin[d], 0, WID, peers(d), 2.6, NE)
-    for d in cores:
-        if halfin[d]:
-            h = msgs[halfin[d][0]]
-            add(d, halfin[d], h["c0"], h["c1"], peers(d), 3.0, NE)
+                    at.setdefault((d, kk), []).append(m)
+    got = {c: [] for c in cores}
+    for X in chips:
+        for k in range(2):
+            o = own[X][k]
+            free = [own[Y][k] for Y in chips if Y != X and own[Y][k] not in shut[X, k]]
+            for src, parts, dsts, stage in ((o, ["x"] + at[o, k], free, 2.0),
+                                            (helper.get((X, k)), at.get((helper.get((X, k)), k)), shut[X, k], 2.5)):
+                if dsts:
+                    m = add(src, parts, k, dsts, stage)
+                    for d in dsts:
+                        got[d].append(m)
+    for X in chips:
+        for k in range(2):
+            add(own[X][k], ["x"] + got[own[X][k]], k, [own[X][1 - k]], 3.0)
     assert len(msgs) <= NSLOT
     return msgs
 
@@ -101,18 +83,16 @@ def rank_program(g, core, T, topo):
     def msem(i):
         return sem["m%d" % i]
 
-    def piece(p, c0, c1):
-        return T.xs[:, c0:c1] if p == "x" else T.land[:, p * WID + c0:p * WID + c1]
+    def piece(p, k):
+        return T.xs[:, k * HALF:(k + 1) * HALF] if p == "x" else T.land[:, p * HALF:(p + 1) * HALF]
 
     if rank is not None:
         g.sync.dma_start(T.xs[:], T.x[:]).then_inc(sem.ldx, 16)
-        g.scalar.dma_start(T.aw[:], T.a[:]).then_inc(sem.lda, 16)
+        g.sync.dma_start(T.aw[:], T.a[:]).then_inc(sem.lda, 16)
 
-    def key(m):
-        return 1.0 if m["stage"] < 2 else m["stage"]
     seen, total = set(), 0
-    for k in sorted({key(m) for m in mine}):
-        grp = [m for m in mine if key(m) == k]
+    for st in sorted({m["stage"] for m in mine}):
+        grp = [m for m in mine if m["stage"] == st]
         for m in grp:
             for p in m["parts"]:
                 if p not in seen:
@@ -122,21 +102,19 @@ def rank_program(g, core, T, topo):
                     else:
                         g.wait_ge(msem(p), msgs[p]["ne"])
         used, trs = set(), []
-        for m in sorted(grp, key=lambda m: all(topo.chip(d) == topo.chip(core) for d in m["dsts"])):
+        for m in grp:
             allowed = None
             for d in m["dsts"]:
                 assert topo.may_write(core, d)
                 allowed = topo.mask(core, d) if allowed is None else allowed & topo.mask(core, d)
-            idle = [b for b in range(allowed.bit_length()) if (allowed >> b) & 1 and b not in used]
-            local = all(topo.chip(d) == topo.chip(core) for d in m["dsts"])
-            sel = idle[-m["ne"]:] if local else idle[:m["ne"]]
+            sel = [b for b in range(allowed.bit_length()) if (allowed >> b) & 1 and b not in used][:m["ne"]]
             assert len(sel) == m["ne"]
             used.update(sel)
-            srcs = [piece(p, m["c0"], m["c1"]) for p in m["parts"]]
+            srcs = [piece(p, m["k"]) for p in m["parts"]]
             trs.append(RemoteDMATransfer(
                 dst_ids=[DstId(rid=topo.addr(d)[0], pnc=topo.addr(d)[1]) for d in m["dsts"]],
                 dma_engine_mask=sum(1 << b for b in sel), remote_sem=msem(m["id"]), srcs=srcs,
-                dsts=[piece(m["id"], m["c0"], m["c1"]) for d in m["dsts"]], alu_op=1 if len(srcs) > 1 else 0))
+                dsts=[piece(m["id"], m["k"]) for d in m["dsts"]], alu_op=1 if len(srcs) > 1 else 0))
             total += m["ne"]
         g.remote_dma_fused(trs, local_sem=sem.sent)
 
@@ -145,21 +123,17 @@ def rank_program(g, core, T, topo):
         assert all(coef[j] == 1 for j in range(len(cores)) if j != rank) and coef[rank] >= 1
         jobs = [(None, "x", b) for _ in range(coef[rank]) for b in range(2)]
         for m in sorted((m for m in msgs if core in m["dsts"]), key=lambda m: (m["stage"], m["id"])):
-            for b in range(2):
-                if m["c0"] <= b * HALF and (b + 1) * HALF <= m["c1"]:
-                    jobs.append((m, m["id"], b))
+            jobs.append((m, m["id"], m["k"]))
         ps = [T.ps0, T.ps1]
         count = [sum(1 for j in jobs if j[2] == b) for b in range(2)]
-        done, waited, order = [0, 0], set(), []
+        done, order = [0, 0], []
         t = g.tensor
         t.wait_ge(sem.lda, 16)
         t.wait_ge(sem.ldx, 16)
         for m, p, b in jobs:
-            if m is not None and p not in waited:
-                waited.add(p)
+            if m is not None:
                 t.wait_ge(msem(p), m["ne"])
-            ins = t.matmul(ps[b][:, 0:HALF], T.aw[:], piece(p, b * HALF, (b + 1) * HALF),
-                           done[b] == 0, done[b] == count[b] - 1)
+            ins = t.matmul(ps[b][:, 0:HALF], T.aw[:], piece(p, b), done[b] == 0, done[b] == count[b] - 1)
             done[b] += 1
             if done[b] == count[b]:
                 ins.then_inc(sem["mm%d" % b], 1)

@@ -2,7 +2,7 @@ from concourse.bass import DstId, RemoteDMATransfer
 
 WID = 512
 HALF = 256
-NSLOT = 32
+NSLOT = 40
 
 SCRATCH = {
     "xs": ("sbuf", [128, WID], "bfloat16"),
@@ -22,6 +22,10 @@ def make_plan(cores, topo):
                for X in chips)
     msgs = []
 
+    def after(X):
+        i = chips.index(X)
+        return chips[i + 1:] + chips[:i]
+
     def engines(src, dsts):
         m = None
         for d in dsts:
@@ -37,7 +41,7 @@ def make_plan(cores, topo):
     for X in chips:
         for k in range(2):
             o = own[X][k]
-            shut[X, k] = [own[Y][k] for Y in chips if Y != X and not topo.may_write(o, own[Y][k])]
+            shut[X, k] = [own[Y][k] for Y in after(X) if not topo.may_write(o, own[Y][k])]
             if shut[X, k]:
                 helper[X, k] = next(h for h in range(topo.CHIPS * topo.CORES_PER_CHIP)
                                     if topo.chip(h) == X and h not in cores and topo.die(h) == topo.die(o)
@@ -46,27 +50,37 @@ def make_plan(cores, topo):
     for X in chips:
         for k in range(2):
             s = own[X][k]
-            outs = [(1 - k, [own[X][1 - k]] + ([helper[X, 1 - k]] if (X, 1 - k) in helper else []))]
+            outs = [(1 - k, ([helper[X, 1 - k]] if (X, 1 - k) in helper else []) + [own[X][1 - k]])]
             if (X, k) in helper:
                 outs.append((k, [helper[X, k]]))
             for kk, dsts in outs:
                 m = add(s, ["x"], kk, dsts, 1.0, len(outs))
                 for d in dsts:
                     at.setdefault((d, kk), []).append(m)
-    got = {c: [] for c in cores}
+    early, late = {c: [] for c in cores}, {c: [] for c in cores}
     for X in chips:
         for k in range(2):
             o = own[X][k]
-            free = [own[Y][k] for Y in chips if Y != X and own[Y][k] not in shut[X, k]]
-            for src, parts, dsts, stage in ((o, ["x"] + at[o, k], free, 2.0),
-                                            (helper.get((X, k)), at.get((helper.get((X, k)), k)), shut[X, k], 2.5)):
+            free = [own[Y][k] for Y in after(X) if own[Y][k] not in shut[X, k]]
+            for src, parts, dsts, stage, box in (
+                    (o, ["x"] + at[o, k], free, 2.0, early),
+                    (helper.get((X, k)), at.get((helper.get((X, k)), k)), shut[X, k], 2.5, late)):
                 if dsts:
                     m = add(src, parts, k, dsts, stage)
                     for d in dsts:
-                        got[d].append(m)
+                        box[d].append(m)
     for X in chips:
         for k in range(2):
-            add(own[X][k], ["x"] + got[own[X][k]], k, [own[X][1 - k]], 3.0)
+            o, p = own[X][k], own[X][1 - k]
+            first, last = early[o], late[o]
+            if first and not last:
+                first = sorted(first, key=lambda m: msgs[m]["dsts"].index(o))
+                first, last = first[:-1], first[-1:]
+            if first and last:
+                add(o, ["x"] + first, k, [p], 2.8)
+                add(o, last, k, [p], 3.0)
+            else:
+                add(o, ["x"] + first + last, k, [p], 3.0)
     assert len(msgs) <= NSLOT
     return msgs
 
@@ -122,7 +136,8 @@ def rank_program(g, core, T, topo):
         coef = T.tables["COEF"][rank]
         assert all(coef[j] == 1 for j in range(len(cores)) if j != rank) and coef[rank] >= 1
         jobs = [(None, "x", b) for _ in range(coef[rank]) for b in range(2)]
-        for m in sorted((m for m in msgs if core in m["dsts"]), key=lambda m: (m["stage"], m["id"])):
+        for m in sorted((m for m in msgs if core in m["dsts"]),
+                        key=lambda m: (m["stage"] + 0.1 * m["dsts"].index(core), m["id"])):
             jobs.append((m, m["id"], m["k"]))
         ps = [T.ps0, T.ps1]
         count = [sum(1 for j in jobs if j[2] == b) for b in range(2)]

@@ -2,17 +2,18 @@ from concourse.bass import DstId, RemoteDMATransfer
 
 WID = 512
 HALF = 256
-NSLOT = 40
+NSLOT = 48
+NBLK = 4
 
 SCRATCH = {
     "xs": ("sbuf", [128, WID], "bfloat16"),
     "aw": ("sbuf", [128, 128], "bfloat16"),
     "land": ("sbuf", [128, NSLOT * HALF], "bfloat16"),
     "yb": ("sbuf", [128, WID], "bfloat16"),
-    "ps0": ("psum", [128, 512], "float32"),
-    "ps1": ("psum", [128, 512], "float32"),
 }
-SEMAPHORES = ["ldx", "lda", "sent", "mm0", "mm1", "cp0", "cp1", "st0", "st1"] + ["m%d" % i for i in range(NSLOT)]
+SCRATCH.update({"ps%d" % i: ("psum", [128, 512], "float32") for i in range(NBLK + 1)})
+SEMAPHORES = (["ldx0", "ldx1", "lda", "sent", "cp0", "cp1", "st0", "st1"] + ["mm%d" % i for i in range(NBLK + 1)]
+              + ["m%d" % i for i in range(NSLOT)])
 
 
 def make_plan(cores, topo):
@@ -26,35 +27,39 @@ def make_plan(cores, topo):
         i = chips.index(X)
         return chips[i + 1:] + chips[:i]
 
-    def engines(src, dsts):
+    def add(src, parts, k, dsts, stage, part=None):
         m = None
         for d in dsts:
             m = topo.mask(src, d) if m is None else m & topo.mask(src, d)
-        return bin(m).count("1")
-
-    def add(src, parts, k, dsts, stage, share=1):
+        if part is not None:
+            away = topo.mask(src, next(c for c in cores if topo.chip(c) != topo.chip(src)))
+            m = m & away if part else m & ~away
         msgs.append(dict(id=len(msgs), src=src, parts=list(parts), k=k, dsts=list(dsts), stage=stage,
-                         ne=engines(src, dsts) // share))
+                         mask=m, ne=bin(m).count("1")))
         return len(msgs) - 1
 
-    shut, helper = {}, {}
+    shut, helpers = {}, {}
     for X in chips:
         for k in range(2):
             o = own[X][k]
             shut[X, k] = [own[Y][k] for Y in after(X) if not topo.may_write(o, own[Y][k])]
+            helpers[X, k] = []
             if shut[X, k]:
-                helper[X, k] = next(h for h in range(topo.CHIPS * topo.CORES_PER_CHIP)
-                                    if topo.chip(h) == X and h not in cores and topo.die(h) == topo.die(o)
-                                    and all(topo.may_write(h, d) for d in shut[X, k]))
+                cand = [h for h in range(topo.CHIPS * topo.CORES_PER_CHIP)
+                        if topo.chip(h) == X and h not in cores and topo.die(h) == topo.die(o)
+                        and all(topo.may_write(h, d) for d in shut[X, k])]
+                if len(shut[X, k]) > 2 and len(cand) > 1:
+                    helpers[X, k] = [(cand[0], shut[X, k][:2]), (cand[1], shut[X, k][2:])]
+                else:
+                    helpers[X, k] = [(cand[0], shut[X, k])]
     at = {}
     for X in chips:
         for k in range(2):
             s = own[X][k]
-            outs = [(1 - k, ([helper[X, 1 - k]] if (X, 1 - k) in helper else []) + [own[X][1 - k]])]
-            if (X, k) in helper:
-                outs.append((k, [helper[X, k]]))
-            for kk, dsts in outs:
-                m = add(s, ["x"], kk, dsts, 1.0, len(outs))
+            outs = [(kk, [h for h, _ in helpers[X, kk]]) for kk in (k, 1 - k) if helpers[X, kk]]
+            outs.append((1 - k, [own[X][1 - k]]))
+            for i, (kk, dsts) in enumerate(outs):
+                m = add(s, ["x"], kk, dsts, 1.0 + 0.1 * i, None if len(outs) == 1 else i < len(outs) - 1)
                 for d in dsts:
                     at.setdefault((d, kk), []).append(m)
     early, late = {c: [] for c in cores}, {c: [] for c in cores}
@@ -62,9 +67,9 @@ def make_plan(cores, topo):
         for k in range(2):
             o = own[X][k]
             free = [own[Y][k] for Y in after(X) if own[Y][k] not in shut[X, k]]
-            for src, parts, dsts, stage, box in (
-                    (o, ["x"] + at[o, k], free, 2.0, early),
-                    (helper.get((X, k)), at.get((helper.get((X, k)), k)), shut[X, k], 2.5, late)):
+            jobs = [(o, ["x"] + at[o, k], free, 2.0, early)]
+            jobs += [(h, at[h, k], ds, 2.5, late) for h, ds in helpers[X, k]]
+            for src, parts, dsts, stage, box in jobs:
                 if dsts:
                     m = add(src, parts, k, dsts, stage)
                     for d in dsts:
@@ -76,11 +81,12 @@ def make_plan(cores, topo):
             if first and not last:
                 first = sorted(first, key=lambda m: msgs[m]["dsts"].index(o))
                 first, last = first[:-1], first[-1:]
-            if first and last:
-                add(o, ["x"] + first, k, [p], 2.8)
-                add(o, last, k, [p], 3.0)
-            else:
-                add(o, ["x"] + first + last, k, [p], 3.0)
+            elif last and not first:
+                near = [m for m in last if topo.mates(topo.chip(msgs[m]["src"]), X)]
+                if len(near) < len(last):
+                    first, last = near, [m for m in last if m not in near]
+            add(o, ["x"] + first, k, [p], 2.8)
+            add(o, last, k, [p], 3.0)
     assert len(msgs) <= NSLOT
     return msgs
 
@@ -88,7 +94,7 @@ def make_plan(cores, topo):
 def rank_program(g, core, T, topo):
     cores = list(T.cores)
     msgs = make_plan(cores, topo)
-    mine = [m for m in msgs if m["src"] == core]
+    mine = sorted((m for m in msgs if m["src"] == core), key=lambda m: (m["stage"], m["id"]))
     rank = T.rank_of(core)
     if rank is None and not mine:
         return
@@ -97,67 +103,70 @@ def rank_program(g, core, T, topo):
     def msem(i):
         return sem["m%d" % i]
 
-    def piece(p, k):
-        return T.xs[:, k * HALF:(k + 1) * HALF] if p == "x" else T.land[:, p * HALF:(p + 1) * HALF]
+    def piece(p, k, off=0, w=HALF):
+        if p == "x":
+            return T.xs[:, k * HALF + off:k * HALF + off + w]
+        return T.land[:, p * HALF + off:p * HALF + off + w]
 
     if rank is not None:
-        g.sync.dma_start(T.xs[:], T.x[:]).then_inc(sem.ldx, 16)
+        k0 = mine[0]["k"]
+        for k in (k0, 1 - k0):
+            cols = slice(k * HALF, (k + 1) * HALF)
+            g.sync.dma_start(T.xs[:, cols], T.x[:, cols]).then_inc(sem["ldx%d" % k], 16)
         g.sync.dma_start(T.aw[:], T.a[:]).then_inc(sem.lda, 16)
 
     seen, total = set(), 0
-    for st in sorted({m["stage"] for m in mine}):
-        grp = [m for m in mine if m["stage"] == st]
-        for m in grp:
-            for p in m["parts"]:
-                if p not in seen:
-                    seen.add(p)
-                    if p == "x":
-                        g.wait_ge(sem.ldx, 16)
-                    else:
-                        g.wait_ge(msem(p), msgs[p]["ne"])
-        used, trs = set(), []
-        for m in grp:
-            allowed = None
-            for d in m["dsts"]:
-                assert topo.may_write(core, d)
-                allowed = topo.mask(core, d) if allowed is None else allowed & topo.mask(core, d)
-            sel = [b for b in range(allowed.bit_length()) if (allowed >> b) & 1 and b not in used][:m["ne"]]
-            assert len(sel) == m["ne"]
-            used.update(sel)
-            srcs = [piece(p, m["k"]) for p in m["parts"]]
-            trs.append(RemoteDMATransfer(
-                dst_ids=[DstId(rid=topo.addr(d)[0], pnc=topo.addr(d)[1]) for d in m["dsts"]],
-                dma_engine_mask=sum(1 << b for b in sel), remote_sem=msem(m["id"]), srcs=srcs,
-                dsts=[piece(m["id"], m["k"]) for d in m["dsts"]], alu_op=1 if len(srcs) > 1 else 0))
-            total += m["ne"]
-        g.remote_dma_fused(trs, local_sem=sem.sent)
+    for m in mine:
+        for p in m["parts"]:
+            if (p, m["k"]) not in seen:
+                seen.add((p, m["k"]))
+                if p == "x":
+                    g.wait_ge(sem["ldx%d" % m["k"]], 16)
+                else:
+                    g.wait_ge(msem(p), msgs[p]["ne"])
+        srcs = [piece(p, m["k"]) for p in m["parts"]]
+        assert all(topo.may_write(core, d) for d in m["dsts"])
+        g.remote_dma_fused([RemoteDMATransfer(
+            dst_ids=[DstId(rid=topo.addr(d)[0], pnc=topo.addr(d)[1]) for d in m["dsts"]],
+            dma_engine_mask=m["mask"], remote_sem=msem(m["id"]), srcs=srcs,
+            dsts=[piece(m["id"], m["k"]) for d in m["dsts"]], alu_op=1 if len(srcs) > 1 else 0)],
+            local_sem=sem.sent)
+        total += m["ne"]
 
     if rank is not None:
         coef = T.tables["COEF"][rank]
         assert all(coef[j] == 1 for j in range(len(cores)) if j != rank) and coef[rank] >= 1
+        kk = mine[-1]["k"]
+        w = HALF // NBLK
+        blocks = {kk: [(T.ps0, 0, HALF, "mm0")],
+                  1 - kk: [(T["ps%d" % (i + 1)], i * w, w, "mm%d" % (i + 1)) for i in range(NBLK)]}
         jobs = [(None, "x", b) for _ in range(coef[rank]) for b in range(2)]
         for m in sorted((m for m in msgs if core in m["dsts"]),
                         key=lambda m: (m["stage"] + 0.1 * m["dsts"].index(core), m["id"])):
             jobs.append((m, m["id"], m["k"]))
-        ps = [T.ps0, T.ps1]
         count = [sum(1 for j in jobs if j[2] == b) for b in range(2)]
         done, order = [0, 0], []
         t = g.tensor
         t.wait_ge(sem.lda, 16)
-        t.wait_ge(sem.ldx, 16)
+        t.wait_ge(sem.ldx0, 16)
+        t.wait_ge(sem.ldx1, 16)
         for m, p, b in jobs:
             if m is not None:
                 t.wait_ge(msem(p), m["ne"])
-            ins = t.matmul(ps[b][:, 0:HALF], T.aw[:], piece(p, b), done[b] == 0, done[b] == count[b] - 1)
             done[b] += 1
+            for ps, off, wd, ms in blocks[b]:
+                ins = t.matmul(ps[:, 0:wd], T.aw[:], piece(p, b, off, wd), done[b] == 1, done[b] == count[b])
+                if done[b] == count[b]:
+                    ins.then_inc(sem[ms], 1)
             if done[b] == count[b]:
-                ins.then_inc(sem["mm%d" % b], 1)
                 order.append(b)
         for q, b in zip((g.sync, g.scalar), order):
+            for ps, off, wd, ms in blocks[b]:
+                g.vector.wait_ge(sem[ms], 1)
+                g.vector.tensor_copy(T.yb[:, b * HALF + off:b * HALF + off + wd],
+                                     ps[:, 0:wd]).then_inc(sem["cp%d" % b], 1)
             cols = slice(b * HALF, (b + 1) * HALF)
-            g.vector.wait_ge(sem["mm%d" % b], 1)
-            g.vector.tensor_copy(T.yb[:, cols], ps[b][:, 0:HALF]).then_inc(sem["cp%d" % b], 1)
-            q.wait_ge(sem["cp%d" % b], 1)
+            q.wait_ge(sem["cp%d" % b], len(blocks[b]))
             q.dma_start(T.y[:, cols], T.yb[:, cols]).then_inc(sem["st%d" % b], 16)
     if total:
         g.wait_ge(sem.sent, total)

from concourse.bass import DstId, RemoteDMATransfer

WID = 512
HALF = 256
NSLOT = 48
NBLK = 4

SCRATCH = {
    "xs": ("sbuf", [128, WID], "bfloat16"),
    "aw": ("sbuf", [128, 128], "bfloat16"),
    "land": ("sbuf", [128, NSLOT * HALF], "bfloat16"),
    "yb": ("sbuf", [128, WID], "bfloat16"),
}
SCRATCH.update({"ps%d" % i: ("psum", [128, 512], "float32") for i in range(NBLK + 1)})
SEMAPHORES = (["ldx0", "ldx1", "lda", "sent", "cp0", "cp1", "st0", "st1"] + ["mm%d" % i for i in range(NBLK + 1)]
              + ["m%d" % i for i in range(NSLOT)])


def make_plan(cores, topo):
    chips = sorted({topo.chip(c) for c in cores})
    own = {X: sorted((c for c in cores if topo.chip(c) == X), key=topo.die) for X in chips}
    assert all(len(own[X]) == 2 and [topo.die(c) for c in own[X]] == [topo.die(c) for c in own[chips[0]]]
               for X in chips)
    msgs = []

    def after(X):
        i = chips.index(X)
        return chips[i + 1:] + chips[:i]

    def add(src, parts, k, dsts, stage, part=None):
        m = None
        for d in dsts:
            m = topo.mask(src, d) if m is None else m & topo.mask(src, d)
        if part is not None:
            away = topo.mask(src, next(c for c in cores if topo.chip(c) != topo.chip(src)))
            m = m & away if part else m & ~away
        msgs.append(dict(id=len(msgs), src=src, parts=list(parts), k=k, dsts=list(dsts), stage=stage,
                         mask=m, ne=bin(m).count("1")))
        return len(msgs) - 1

    shut, helpers = {}, {}
    for X in chips:
        for k in range(2):
            o = own[X][k]
            shut[X, k] = [own[Y][k] for Y in after(X) if not topo.may_write(o, own[Y][k])]
            helpers[X, k] = []
            if shut[X, k]:
                cand = [h for h in range(topo.CHIPS * topo.CORES_PER_CHIP)
                        if topo.chip(h) == X and h not in cores and topo.die(h) == topo.die(o)
                        and all(topo.may_write(h, d) for d in shut[X, k])]
                if len(shut[X, k]) > 2 and len(cand) > 1:
                    helpers[X, k] = [(cand[0], shut[X, k][:2]), (cand[1], shut[X, k][2:])]
                else:
                    helpers[X, k] = [(cand[0], shut[X, k])]
    at = {}
    for X in chips:
        for k in range(2):
            s = own[X][k]
            outs = [(kk, [h for h, _ in helpers[X, kk]]) for kk in (k, 1 - k) if helpers[X, kk]]
            outs.append((1 - k, [own[X][1 - k]]))
            for i, (kk, dsts) in enumerate(outs):
                m = add(s, ["x"], kk, dsts, 1.0 + 0.1 * i, None if len(outs) == 1 else i < len(outs) - 1)
                for d in dsts:
                    at.setdefault((d, kk), []).append(m)
    early, late = {c: [] for c in cores}, {c: [] for c in cores}
    for X in chips:
        for k in range(2):
            o = own[X][k]
            free = [own[Y][k] for Y in after(X) if own[Y][k] not in shut[X, k]]
            jobs = [(o, ["x"] + at[o, k], free, 2.0, early)]
            jobs += [(h, at[h, k], ds, 2.5, late) for h, ds in helpers[X, k]]
            for src, parts, dsts, stage, box in jobs:
                if dsts:
                    m = add(src, parts, k, dsts, stage)
                    for d in dsts:
                        box[d].append(m)
    for X in chips:
        for k in range(2):
            o, p = own[X][k], own[X][1 - k]
            first, last = early[o], late[o]
            if first and not last:
                first = sorted(first, key=lambda m: msgs[m]["dsts"].index(o))
                first, last = first[:-1], first[-1:]
            elif last and not first:
                near = [m for m in last if topo.mates(topo.chip(msgs[m]["src"]), X)]
                if len(near) < len(last):
                    first, last = near, [m for m in last if m not in near]
            add(o, ["x"] + first, k, [p], 2.8)
            add(o, last, k, [p], 3.0)
    assert len(msgs) <= NSLOT
    return msgs


def rank_program(g, core, T, topo):
    cores = list(T.cores)
    msgs = make_plan(cores, topo)
    mine = sorted((m for m in msgs if m["src"] == core), key=lambda m: (m["stage"], m["id"]))
    rank = T.rank_of(core)
    if rank is None and not mine:
        return
    sem = T.sem

    def msem(i):
        return sem["m%d" % i]

    def piece(p, k, off=0, w=HALF):
        if p == "x":
            return T.xs[:, k * HALF + off:k * HALF + off + w]
        return T.land[:, p * HALF + off:p * HALF + off + w]

    if rank is not None:
        k0 = mine[0]["k"]
        for k in (k0, 1 - k0):
            cols = slice(k * HALF, (k + 1) * HALF)
            g.sync.dma_start(T.xs[:, cols], T.x[:, cols]).then_inc(sem["ldx%d" % k], 16)
        g.sync.dma_start(T.aw[:], T.a[:]).then_inc(sem.lda, 16)

    seen, total = set(), 0
    for m in mine:
        for p in m["parts"]:
            if (p, m["k"]) not in seen:
                seen.add((p, m["k"]))
                if p == "x":
                    g.wait_ge(sem["ldx%d" % m["k"]], 16)
                else:
                    g.wait_ge(msem(p), msgs[p]["ne"])
        srcs = [piece(p, m["k"]) for p in m["parts"]]
        assert all(topo.may_write(core, d) for d in m["dsts"])
        g.remote_dma_fused([RemoteDMATransfer(
            dst_ids=[DstId(rid=topo.addr(d)[0], pnc=topo.addr(d)[1]) for d in m["dsts"]],
            dma_engine_mask=m["mask"], remote_sem=msem(m["id"]), srcs=srcs,
            dsts=[piece(m["id"], m["k"]) for d in m["dsts"]], alu_op=1 if len(srcs) > 1 else 0)],
            local_sem=sem.sent)
        total += m["ne"]

    if rank is not None:
        coef = T.tables["COEF"][rank]
        assert all(coef[j] == 1 for j in range(len(cores)) if j != rank) and coef[rank] >= 1
        kk = mine[-1]["k"]
        w = HALF // NBLK
        blocks = {kk: [(T.ps0, 0, HALF, "mm0")],
                  1 - kk: [(T["ps%d" % (i + 1)], i * w, w, "mm%d" % (i + 1)) for i in range(NBLK)]}
        jobs = [(None, "x", b) for _ in range(coef[rank]) for b in range(2)]
        for m in sorted((m for m in msgs if core in m["dsts"]),
                        key=lambda m: (m["stage"] + 0.1 * m["dsts"].index(core), m["id"])):
            jobs.append((m, m["id"], m["k"]))
        count = [sum(1 for j in jobs if j[2] == b) for b in range(2)]
        done, order = [0, 0], []
        t = g.tensor
        t.wait_ge(sem.lda, 16)
        t.wait_ge(sem.ldx0, 16)
        t.wait_ge(sem.ldx1, 16)
        for m, p, b in jobs:
            if m is not None:
                t.wait_ge(msem(p), m["ne"])
            done[b] += 1
            for ps, off, wd, ms in blocks[b]:
                ins = t.matmul(ps[:, 0:wd], T.aw[:], piece(p, b, off, wd), done[b] == 1, done[b] == count[b])
                if done[b] == count[b]:
                    ins.then_inc(sem[ms], 1)
            if done[b] == count[b]:
                order.append(b)
        for q, b in zip((g.sync, g.scalar), order):
            for ps, off, wd, ms in blocks[b]:
                g.vector.wait_ge(sem[ms], 1)
                g.vector.tensor_copy(T.yb[:, b * HALF + off:b * HALF + off + wd],
                                     ps[:, 0:wd]).then_inc(sem["cp%d" % b], 1)
            cols = slice(b * HALF, (b + 1) * HALF)
            q.wait_ge(sem["cp%d" % b], len(blocks[b]))
            q.dma_start(T.y[:, cols], T.yb[:, cols]).then_inc(sem["st%d" % b], 16)
    if total:
        g.wait_ge(sem.sent, total)
    if rank is not None:
        g.wait_ge(sem.st0, 16)
        g.wait_ge(sem.st1, 16)
